import numpy as np
import ml_dtypes


def mxq(x, axis, fmt="e4m3"):
    dtype, down = {"e4m3": (ml_dtypes.float8_e4m3fn, 7), "e5m2": (ml_dtypes.float8_e5m2, 14)}[fmt]
    v = np.moveaxis(np.asarray(x, np.float32).astype(ml_dtypes.bfloat16).astype(np.float64), axis, -1)
    blocks = v.reshape(v.shape[:-1] + (-1, 32))
    amax = np.abs(blocks).max(-1, keepdims=True)
    byte = np.maximum(np.where(amax > 0, np.frexp(amax)[1] - 1 + 127, 0) - down, 1)
    scale = np.exp2(byte - 127.0)
    codes = (blocks / scale).astype(np.float32).astype(dtype).astype(np.float64)
    return np.moveaxis((codes * scale).reshape(v.shape), -1, axis)


WIDE = False


def mx_kscale(k):
    if not WIDE:
        return np.ones(k)
    levels = np.array([10, -10, 5, -5, 0])
    if k % 512:
        return np.exp2(np.random.permutation(np.resize(levels, k // 32))).repeat(32)
    a = np.empty((k // 512, 16))
    for p in range(k // 512):
        a[p, :8] = np.random.permutation(np.resize(levels, 8))
        for g in range(8):
            far = levels[np.abs(levels - a[p, g]) >= 10]
            a[p, g + 8] = far[np.random.randint(len(far))]
    return np.exp2(a.ravel()).repeat(32)


def f64(x):
    return np.asarray(x).astype(np.float64)


def striped(idx):
    return np.tile(idx.reshape(-1, 16).T, (8, 1)).astype(np.uint16)


def unstriped(offs):
    return offs[:16].T.reshape(-1).astype(np.int64)


def striped8(idx):
    return np.concatenate([x.reshape(-1, 16).T for x in idx]).astype(np.uint16)


def runs(offs, k):
    lists = np.stack([offs[16 * r : 16 * r + 16].T.reshape(-1) for r in range(8)]).astype(np.int64)
    return lists[np.arange(k) % 512 // 64]


def pack_weight(w):
    k, n = w.shape
    w = f64(np.asarray(w, np.float32).astype(ml_dtypes.bfloat16)).reshape(k // 32, 32, n)
    amax = np.abs(w).max(1)
    byte = np.clip(np.where(amax > 0, np.frexp(amax)[1] - 1 + 127 - 7, 1), 1, 254)
    scaled = (w * np.exp2(127.0 - byte)[:, None, :]).reshape(k, n).astype(np.float32)
    words = np.ascontiguousarray(scaled.reshape(k // 512, 128, 4, n).transpose(0, 1, 3, 2)).astype(ml_dtypes.float8_e4m3fn).view(np.uint8)
    return words, np.ascontiguousarray(byte.astype(np.uint8).reshape(k // 512, 16, n))


def unpack_weight(words, scales):
    g, p, n, _ = words.shape
    vals = np.ascontiguousarray(words).view(ml_dtypes.float8_e4m3fn).astype(np.float64) * np.repeat(np.exp2(scales.astype(np.float64) - 127.0), 8, axis=1)[..., None]
    return vals.transpose(0, 1, 3, 2).reshape(g * 512, n)


E2M1 = np.array([0.0, 0.5, 1.0, 1.5, 2.0, 3.0, 4.0, 6.0, -0.0, -0.5, -1.0, -1.5, -2.0, -3.0, -4.0, -6.0])


def pack_fp4(w):
    k, n = w.shape
    w = f64(np.asarray(w, np.float32).astype(ml_dtypes.bfloat16)).reshape(k // 32, 32, n)
    amax = np.abs(w).max(1)
    mant, ex = np.frexp(amax / 6.0)
    byte = np.clip(np.where(amax > 0, np.where(mant > 0.5, ex, ex - 1) + 127, 1), 1, 254)
    scaled = (w * np.exp2(127.0 - byte)[:, None, :]).reshape(k, n).astype(np.float32)
    c = np.ascontiguousarray(scaled.reshape(k // 512, 128, 4, n).transpose(0, 1, 3, 2)).astype(ml_dtypes.float4_e2m1fn).view(np.uint8) & 0xF
    words = (c[..., 0::2] | (c[..., 1::2] << 4)).reshape(k // 512, 128, 2 * n)
    return np.ascontiguousarray(words), np.ascontiguousarray(byte.astype(np.uint8).reshape(k // 512, 16, n))


def unpack_fp4(words, scales):
    g, _, n = scales.shape
    words = np.ascontiguousarray(words).reshape(g, 128, n, 2)
    nib = np.empty((g, 128, n, 4), np.uint8)
    nib[..., 0::2] = words & 0xF
    nib[..., 1::2] = words >> 4
    vals = E2M1[nib] * np.repeat(np.exp2(scales.astype(np.float64) - 127.0), 8, axis=1)[..., None]
    return vals.transpose(0, 1, 3, 2).reshape(g * 512, n)


def sigmoid(v):
    return 1.0 / (1.0 + np.exp(-np.maximum(v, -700.0)))


K, T, S, N, G, H, W = 512, 1024, 256, 512, 2048, 512, 128


def setup_inputs():
    n = np.random.standard_normal
    s = mx_kscale(K)[:, None]
    u = mx_kscale(K)
    packed_xT = pack_weight(n((K, T)) * s)
    packed_dT = pack_weight(n((K, G)) / s)
    packed_w1 = pack_fp4(n((H, N)) / np.sqrt(H) / u[:, None])
    perm = np.random.permutation(S)
    perm2 = np.random.permutation(S)
    return {
        "x_words": packed_xT[0],
        "x_scales": packed_xT[1],
        "d_words": packed_dT[0],
        "d_scales": packed_dT[1],
        "gn": (np.random.uniform(0.5, 1.5, (H, 1)) * u[:, None]).astype(np.float32),
        "w1_words": packed_w1[0],
        "w1_scales": packed_w1[1],
        "sl": np.random.uniform(1.0, 2.0, (N, 1)).astype(np.float32),
        "th": (0.5 * n((N, 1))).astype(np.float32),
        "offs": striped(np.random.permutation(T)[:S]),
        "k1": striped8(np.random.randint(0, G, (8, H))),
        "two": striped(np.random.permutation(T)[:S]),
        "k2": striped8(np.random.randint(0, G, (8, H))),
        "n1": striped(np.random.permutation(S)),
        "n2": striped(perm[:W]),
        "n3": striped(perm[W:]),
        "n4": striped(perm2[:W]),
        "n5": striped(perm2[W:]),
    }


def reference(x_words, x_scales, d_words, d_scales, gn, w1_words, w1_scales, sl, th, offs, k1, two, k2, n1, n2, n3, n4, n5):
    d_k1 = unpack_weight(d_words, d_scales)[np.arange(K)[:, None], runs(k1, K)]
    xq = unpack_weight(x_words, x_scales)[:, unstriped(offs)]
    d_k2 = unpack_weight(d_words, d_scales)[np.arange(K)[:, None], runs(k2, K)]
    x_two = unpack_weight(x_words, x_scales)[:, unstriped(two)]
    h = 0.0625 * (d_k1.T @ xq + d_k2.T @ x_two)
    z = f64(gn) * h
    h2 = unpack_fp4(w1_words, w1_scales).T @ mxq(z, 0, "e4m3")
    sg = sigmoid(f64(sl) * (h2[:, unstriped(n1)] - f64(th)))
    st = h2 * sg
    pa = st[:, unstriped(n2)]
    pb = st[:, unstriped(n3)]
    rb = pa - pb
    ra = np.maximum(pa, pb)
    ua = np.zeros((N, S))
    ua[:, unstriped(n4)] = ra
    out = ua.copy()
    out[:, unstriped(n5)] = rb
    return out

@@ -1,0 +1,209 @@
+from contextlib import ExitStack
+
+import concourse.mybir as mybir
+
+K, T, S, N, G, H, W = 512, 1024, 256, 512, 2048, 512, 128
+FLOPS = 2 * (2 * K * H * S + H * N * S)
+
+F32 = mybir.dt.float32
+BF16 = mybir.dt.bfloat16
+I32 = mybir.dt.int32
+U32 = mybir.dt.uint32
+U16 = mybir.dt.uint16
+U8 = mybir.dt.uint8
+FP8X4 = mybir.dt.float8_e4m3fn_x4
+FP4X4 = mybir.dt.float4_e2m1fn_x4
+ALU = mybir.AluOpType
+ACT = mybir.ActivationFunctionType
+
+P = 128
+PACK = 4
+HALF = S // 2
+
+
+def tile_picked_mttonecpx_none_p_kernel(
+    tc, x_words, x_scales, d_words, d_scales, gn, w1_words, w1_scales, sl, th,
+    offs, k1, two, k2, n1, n2, n3, n4, n5, out,
+):
+    nc = tc.nc
+    with ExitStack() as ctx:
+        sb = ctx.enter_context(tc.tile_pool(name="sb", bufs=1))
+        ps = ctx.enter_context(tc.psum_pool(name="ps", bufs=1))
+
+        def tile(name, shape, dtype, tag=None):
+            return sb.tile(shape, dtype, name=name, tag=tag or name, align_bytes=64)
+
+        def load_list(name, src):
+            t = tile(name, list(src.shape), U16)
+            nc.sync.dma_start(t[:], src)
+            return t
+
+        def load_rows(queue, plane, rows, q):
+            four = rows[4 * q : 4 * q + 4, :].bitcast(I32)
+            queue.dma_start(plane[32 * q : 32 * (q + 1), :].bitcast(I32), four.unsqueeze(0).to_broadcast([8] + list(four.shape)))
+
+        ds_win = tile("ds_win", [P, G], U8)
+        dw_win = tile("dw_win", [P, G], U32)
+        xs_win = tile("xs_win", [P, T], U8)
+        xw_win = tile("xw_win", [P, T], U32)
+        d_plane = tile("d_plane", [P, 2 * H], U8)
+        nc.vector.memset(d_plane[:].bitcast(I32), 0)
+
+        k1_l = load_list("k1_l", k1)
+        nc.sync.dma_start(
+            ds_win[:].bitcast(I32),
+            d_scales[0].bitcast(I32).unsqueeze(1).to_broadcast([16, 8, G // 4]),
+        )
+        k2_l = load_list("k2_l", k2)
+        load_rows(nc.sync, xs_win, x_scales[0], 0)
+        nc.sync.dma_start(dw_win[:].bitcast(I32), d_words[0].rearrange("p c r -> p (c r)").bitcast(I32))
+        for q in range(1, 4):
+            load_rows(nc.sync, xs_win, x_scales[0], q)
+        offs_l = load_list("offs_l", offs)
+        two_l = load_list("two_l", two)
+        nc.sync.dma_start(xw_win[:].bitcast(I32), x_words[0].rearrange("p c r -> p (c r)").bitcast(I32))
+        n1_l = load_list("n1_l", n1)
+        n2_l = load_list("n2_l", n2)
+        n3_l = load_list("n3_l", n3)
+        n4_l = load_list("n4_l", n4)
+        n5_l = load_list("n5_l", n5)
+        gain = tile("gain", [P, PACK], F32)
+        nc.gpsimd.dma_start(gain[:], gn.rearrange("(p t) o -> p (t o)", t=PACK))
+
+        ds_got = tile("ds_got", [P, 2 * H], U8)
+        nc.vector.tensor_copy(ds_got[:, :H], ds_win[:].indirect(k1_l[:]))
+        nc.vector.tensor_copy(ds_got[:, H:], ds_win[:].indirect(k2_l[:]))
+        ds_dealt = tile("ds_dealt", [P, 2 * H], U8)
+        nc.vector.tensor_copy(
+            ds_dealt[:].rearrange("p (t a b) -> p a t b", t=PACK, b=16),
+            ds_got[:].rearrange("p (a b t) -> p a t b", t=PACK, b=16),
+        )
+        for s in range(4):
+            nc.scalar.dma_start(d_plane[s:P:32, :].bitcast(I32), ds_dealt[8 * s : P : 32, :].bitcast(I32))
+        w1_codes = tile("w1_codes", [P, 2 * N], U8, tag="ds_got")
+        nc.scalar.dma_start(w1_codes[:].bitcast(I32), w1_words[0].bitcast(I32))
+
+        def gather_words(name, lst):
+            got = tile(name + "_got", [P, H], U32)
+            nc.vector.tensor_copy(got[:], dw_win[:].indirect(lst[:]))
+            dealt = tile(name + "_dealt", [P, H], U32)
+            nc.vector.tensor_copy(
+                dealt[:].rearrange("p (t a b) -> p a t b", t=PACK, b=4),
+                got[:].rearrange("p (a b t) -> p a t b", t=PACK, b=4),
+            )
+            return dealt
+
+        xw = [[tile("xw%d%d" % (i, j), [P, HALF], U32) for j in range(2)] for i in range(2)]
+        xs = [[tile("xs%d%d" % (i, j), [P, HALF], U8) for j in range(2)] for i in range(2)]
+        acc = [ps.tile([P, PACK, HALF], F32, name="acc%d" % i) for i in range(2)]
+
+        def product(which, dealt, half):
+            for t in range(PACK):
+                c0 = t * 2 * P + which * P
+                nc.tensor.matmul_mx(
+                    out=acc[half][:, t, :],
+                    lhsT=dealt[:, t * P : (t + 1) * P].bitcast(FP8X4),
+                    lhsT_scale=d_plane[:, c0 : c0 + P],
+                    rhs=xw[which][half][:].bitcast(FP8X4),
+                    rhs_scale=xs[which][half][:],
+                    start=(which == 0 and t == 0),
+                    stop=(which == 1 and t == PACK - 1),
+                )
+
+        dealt = [gather_words("d1", k1_l), gather_words("d2", k2_l)]
+        rowvals = tile("rowvals", [P, 2, 8], F32, tag="d1_got")
+        slope = rowvals[:, 0, 0:4]
+        thresh = rowvals[:, 1, 0:4]
+        with nc.allow_non_contiguous_dma(reason="one value a row, one row a partition"):
+            nc.scalar.dma_start(slope, sl.rearrange("(c p) o -> p (c o)", p=P))
+            nc.scalar.dma_start(thresh, th.rearrange("(c p) o -> p (c o)", p=P))
+        w1_plane = tile("w1_plane", [P, N], U8, tag="ds_dealt")
+        for q in range(4):
+            load_rows(nc.scalar, w1_plane, w1_scales[0], q)
+        for half in range(2):
+            for which, lst in enumerate((offs_l, two_l)):
+                part = lst[:, half * HALF // 16 : (half + 1) * HALF // 16]
+                nc.vector.tensor_copy(xw[which][half][:], xw_win[:].indirect(part))
+                nc.vector.tensor_copy(xs[which][half][:], xs_win[:].indirect(part))
+                product(which, dealt[which], half)
+
+        bias = tile("bias", [P, 4], F32)
+        nc.vector.scalar_tensor_tensor(bias[:], slope, -1.0, thresh, ALU.mult, ALU.mult)
+
+        z = [tile("z%d" % i, [P, HALF, PACK], BF16) for i in range(2)]
+        z_codes = tile("z_codes", [P, S], U32)
+        z_plane = tile("z_plane", [P, S], U8)
+        for half in range(2):
+            nc.vector.scalar_tensor_tensor(
+                z[half][:],
+                acc[half][:].rearrange("p t j -> p j t"),
+                0.0625,
+                gain[:].unsqueeze(1).to_broadcast([P, HALF, PACK]),
+                ALU.mult,
+                ALU.mult,
+            )
+        for half in range(2):
+            cols = slice(half * HALF, (half + 1) * HALF)
+            nc.vector.quantize_mx(
+                out=z_codes[:, cols].bitcast(FP8X4),
+                scales=z_plane[:, cols],
+                in_=z[half][:].rearrange("p j t -> p (j t)"),
+            )
+
+        bank = [ps.tile([P, S], F32, name="bank%d" % i) for i in range(4)]
+
+        def dense(c, cols):
+            nc.tensor.matmul_mx(
+                out=bank[c][:, cols],
+                lhsT=w1_codes[:, 2 * P * c : 2 * P * (c + 1)].bitcast(FP4X4),
+                lhsT_scale=w1_plane[:, P * c : P * (c + 1)],
+                rhs=z_codes[:, cols].bitcast(FP8X4),
+                rhs_scale=z_plane[:, cols],
+                start=True,
+                stop=True,
+            )
+
+        dense(0, slice(0, HALF))
+        dense(0, slice(HALF, S))
+        for c in range(1, 4):
+            dense(c, slice(0, S))
+
+        h2 = [tile("h2_%d" % c, [P, S], F32) for c in range(4)]
+        sg = [tile("sg_%d" % c, [P, S], F32) for c in range(4)]
+        st = [tile("st_%d" % c, [P, S], F32) for c in range(4)]
+        pa = [tile("pa_%d" % c, [P, W], F32) for c in range(4)]
+        pb = [tile("pb_%d" % c, [P, W], F32) for c in range(4)]
+        ra = [tile("ra_%d" % c, [P, W], F32) for c in range(4)]
+        rb = [tile("rb_%d" % c, [P, W], F32) for c in range(4)]
+        res = [tile("res_%d" % c, [P, S], F32) for c in range(4)]
+
+        def gate(c):
+            nc.vector.tensor_copy(h2[c][:], bank[c][:])
+            for half in range(2):
+                nc.scalar.activation(
+                    out=sg[c][:, half * HALF : (half + 1) * HALF],
+                    in_=h2[c][:].indirect(n1_l[:, half * HALF // 16 : (half + 1) * HALF // 16]),
+                    func=ACT.Sigmoid,
+                    scale=rowvals[:, 0, c : c + 1],
+                    bias=bias[:, c : c + 1],
+                )
+            nc.vector.tensor_tensor(st[c][:], h2[c][:], sg[c][:], ALU.mult)
+
+        def pair(c):
+            nc.scalar.activation(out=pa[c][:], in_=st[c][:].indirect(n2_l[:]), func=ACT.Copy)
+            nc.scalar.activation(out=pb[c][:], in_=st[c][:].indirect(n3_l[:]), func=ACT.Copy)
+            nc.vector.tensor_tensor(ra[c][:], pa[c][:], pb[c][:], ALU.max)
+            nc.vector.tensor_tensor(rb[c][:], pa[c][:], pb[c][:], ALU.subtract)
+
+        def place(c):
+            nc.scalar.activation(out=res[c][:].indirect(n4_l[:]), in_=ra[c][:], func=ACT.Copy)
+            nc.scalar.activation(out=res[c][:].indirect(n5_l[:]), in_=rb[c][:], func=ACT.Copy)
+            nc.sync.dma_start(out[c * P : (c + 1) * P, :], res[c][:])
+
+        for step in range(6):
+            if step < 4:
+                gate(step)
+            if 1 <= step < 5:
+                pair(step - 1)
+            if step >= 2:
+                place(step - 2)

@@ -1,6 +1,7 @@
 from contextlib import ExitStack
 
 import concourse.mybir as mybir
+from concourse.masks import make_identity
 
 K, T, S, N, G, H, W = 512, 1024, 256, 512, 2048, 512, 128
 FLOPS = 2 * (2 * K * H * S + H * N * S)
@@ -30,13 +31,22 @@ def tile_picked_mttonecpx_none_p_kernel(
         sb = ctx.enter_context(tc.tile_pool(name="sb", bufs=1))
         ps = ctx.enter_context(tc.psum_pool(name="ps", bufs=1))
 
-        def tile(name, shape, dtype, tag=None):
-            return sb.tile(shape, dtype, name=name, tag=tag or name, align_bytes=64)
+        reuse = ctx.enter_context(tc.tile_pool(name="reuse", bufs=1))
+
+        def tile(name, shape, dtype):
+            return sb.tile(shape, dtype, name=name, align_bytes=64)
+
+        def placed(name, shape, dtype, offset):
+            return reuse.tile(shape, dtype, name=name, align_bytes=64, offset=offset)
 
         def load_list(name, src):
             t = tile(name, list(src.shape), U16)
             nc.sync.dma_start(t[:], src)
             return t
+
+        def load_blocks(win, rows):
+            words = rows.bitcast(I32)
+            nc.sync.dma_start(win[:].bitcast(I32), words.unsqueeze(1).to_broadcast([16, 8, words.shape[1]]))
 
         def load_rows(queue, plane, rows, q):
             four = rows[4 * q : 4 * q + 4, :].bitcast(I32)
@@ -44,105 +54,109 @@ def tile_picked_mttonecpx_none_p_kernel(
 
         ds_win = tile("ds_win", [P, G], U8)
         dw_win = tile("dw_win", [P, G], U32)
+        sc_got = placed("sc_got", [P, 2 * H + 2 * S], U8, 0)
         xs_win = tile("xs_win", [P, T], U8)
         xw_win = tile("xw_win", [P, T], U32)
-        d_plane = tile("d_plane", [P, 2 * H], U8)
-        nc.vector.memset(d_plane[:].bitcast(I32), 0)
+        plane = tile("plane", [P, 2 * H + 2 * S], U8)
+        nc.vector.memset(plane[:].bitcast(I32), 0)
+        gain = tile("gain", [P, PACK], F32)
+        nc.gpsimd.dma_start(gain[:], gn.rearrange("(p t) o -> p (t o)", t=PACK))
+        ident = tile("ident", [P, P], F32)
+        make_identity(nc, ident[:])
 
-        k1_l = load_list("k1_l", k1)
-        nc.sync.dma_start(
-            ds_win[:].bitcast(I32),
-            d_scales[0].bitcast(I32).unsqueeze(1).to_broadcast([16, 8, G // 4]),
-        )
-        k2_l = load_list("k2_l", k2)
-        load_rows(nc.sync, xs_win, x_scales[0], 0)
-        nc.sync.dma_start(dw_win[:].bitcast(I32), d_words[0].rearrange("p c r -> p (c r)").bitcast(I32))
-        for q in range(1, 4):
-            load_rows(nc.sync, xs_win, x_scales[0], q)
         offs_l = load_list("offs_l", offs)
+        load_blocks(xs_win, x_scales[0])
         two_l = load_list("two_l", two)
+        k1_l = load_list("k1_l", k1)
+        load_blocks(ds_win, d_scales[0])
+        k2_l = load_list("k2_l", k2)
         nc.sync.dma_start(xw_win[:].bitcast(I32), x_words[0].rearrange("p c r -> p (c r)").bitcast(I32))
+        nc.sync.dma_start(dw_win[:].bitcast(I32), d_words[0].rearrange("p c r -> p (c r)").bitcast(I32))
         n1_l = load_list("n1_l", n1)
         n2_l = load_list("n2_l", n2)
         n3_l = load_list("n3_l", n3)
         n4_l = load_list("n4_l", n4)
         n5_l = load_list("n5_l", n5)
-        gain = tile("gain", [P, PACK], F32)
-        nc.gpsimd.dma_start(gain[:], gn.rearrange("(p t) o -> p (t o)", t=PACK))
-
-        ds_got = tile("ds_got", [P, 2 * H], U8)
-        nc.vector.tensor_copy(ds_got[:, :H], ds_win[:].indirect(k1_l[:]))
-        nc.vector.tensor_copy(ds_got[:, H:], ds_win[:].indirect(k2_l[:]))
-        ds_dealt = tile("ds_dealt", [P, 2 * H], U8)
-        nc.vector.tensor_copy(
-            ds_dealt[:].rearrange("p (t a b) -> p a t b", t=PACK, b=16),
-            ds_got[:].rearrange("p (a b t) -> p a t b", t=PACK, b=16),
-        )
-        for s in range(4):
-            nc.scalar.dma_start(d_plane[s:P:32, :].bitcast(I32), ds_dealt[8 * s : P : 32, :].bitcast(I32))
-        w1_codes = tile("w1_codes", [P, 2 * N], U8, tag="ds_got")
-        nc.scalar.dma_start(w1_codes[:].bitcast(I32), w1_words[0].bitcast(I32))
-
-        def gather_words(name, lst):
-            got = tile(name + "_got", [P, H], U32)
-            nc.vector.tensor_copy(got[:], dw_win[:].indirect(lst[:]))
-            dealt = tile(name + "_dealt", [P, H], U32)
-            nc.vector.tensor_copy(
-                dealt[:].rearrange("p (t a b) -> p a t b", t=PACK, b=4),
-                got[:].rearrange("p (a b t) -> p a t b", t=PACK, b=4),
-            )
-            return dealt
-
-        xw = [[tile("xw%d%d" % (i, j), [P, HALF], U32) for j in range(2)] for i in range(2)]
-        xs = [[tile("xs%d%d" % (i, j), [P, HALF], U8) for j in range(2)] for i in range(2)]
-        acc = [ps.tile([P, PACK, HALF], F32, name="acc%d" % i) for i in range(2)]
-
-        def product(which, dealt, half):
-            for t in range(PACK):
-                c0 = t * 2 * P + which * P
-                nc.tensor.matmul_mx(
-                    out=acc[half][:, t, :],
-                    lhsT=dealt[:, t * P : (t + 1) * P].bitcast(FP8X4),
-                    lhsT_scale=d_plane[:, c0 : c0 + P],
-                    rhs=xw[which][half][:].bitcast(FP8X4),
-                    rhs_scale=xs[which][half][:],
-                    start=(which == 0 and t == 0),
-                    stop=(which == 1 and t == PACK - 1),
-                )
-
-        dealt = [gather_words("d1", k1_l), gather_words("d2", k2_l)]
-        rowvals = tile("rowvals", [P, 2, 8], F32, tag="d1_got")
+        rowvals = tile("rowvals", [P, 2, 8], F32)
         slope = rowvals[:, 0, 0:4]
         thresh = rowvals[:, 1, 0:4]
         with nc.allow_non_contiguous_dma(reason="one value a row, one row a partition"):
-            nc.scalar.dma_start(slope, sl.rearrange("(c p) o -> p (c o)", p=P))
-            nc.scalar.dma_start(thresh, th.rearrange("(c p) o -> p (c o)", p=P))
-        w1_plane = tile("w1_plane", [P, N], U8, tag="ds_dealt")
+            nc.sync.dma_start(slope, sl.rearrange("(c p) o -> p (c o)", p=P))
+            nc.sync.dma_start(thresh, th.rearrange("(c p) o -> p (c o)", p=P))
+
+        gain_bank = ps.tile([P, PACK, P], F32, name="gain_bank", tag="b0")
+        for t in range(PACK):
+            nc.tensor.transpose(gain_bank[:, t, :], gain[:, t : t + 1].to_broadcast([P, P]), ident[:])
+        gain_row = tile("gain_row", [P, 2, P, 2], F32)
+        nc.scalar.activation(
+            out=gain_row[:], in_=gain_bank[:].rearrange("p (u e) m -> p u m e", e=2), func=ACT.Copy, scale=0.0625
+        )
+
+        nc.vector.tensor_copy(sc_got[:, 2 * H : 2 * H + S], xs_win[:].indirect(offs_l[:]))
+        nc.vector.tensor_copy(sc_got[:, 2 * H + S :], xs_win[:].indirect(two_l[:]))
+        nc.vector.tensor_copy(sc_got[:, :H], ds_win[:].indirect(k1_l[:]))
+        nc.vector.tensor_copy(sc_got[:, H : 2 * H], ds_win[:].indirect(k2_l[:]))
+        for s in range(4):
+            nc.sync.dma_start(plane[s:P:32, :].bitcast(I32), sc_got[8 * s : P : 32, :].bitcast(I32))
+
+        xw = [tile("xw%d" % i, [P, S], U32) for i in range(2)]
+        nc.vector.tensor_copy(xw[0][:], xw_win[:].indirect(offs_l[:]))
+        nc.vector.tensor_copy(xw[1][:], xw_win[:].indirect(two_l[:]))
+        HH = H // 2
+        dw1 = tile("dw1", [P, H], U32)
+        dw2 = [tile("dw2_%d" % i, [P, HH], U32) for i in range(2)]
+        acc = [[ps.tile([P, HH], F32, name="acc%d%d" % (i, j), tag="b%d" % (1 + 2 * i + j)) for j in range(2)] for i in range(2)]
+
+        def product(which, half, part, words):
+            x0 = 2 * H + which * S + half * HALF
+            d0 = which * H + part * HH
+            nc.tensor.matmul_mx(
+                out=acc[half][part][:],
+                lhsT=xw[which][:, half * HALF : (half + 1) * HALF].bitcast(FP8X4),
+                lhsT_scale=plane[:, x0 : x0 + HALF],
+                rhs=words.bitcast(FP8X4),
+                rhs_scale=plane[:, d0 : d0 + HH],
+                start=(which == 0),
+                stop=(which == 1),
+            )
+
+        nc.vector.tensor_copy(dw1[:], dw_win[:].indirect(k1_l[:]))
+        for part in range(2):
+            for half in range(2):
+                product(0, half, part, dw1[:, part * HH : (part + 1) * HH])
+        for part in range(2):
+            nc.vector.tensor_copy(dw2[part][:], dw_win[:].indirect(k2_l[:, part * HH // 16 : (part + 1) * HH // 16]))
+            for half in range(2):
+                product(1, half, part, dw2[part][:])
+
+        w1_plane = placed("w1_plane", [P, N], U8, 0)
+        w1_codes = placed("w1_codes", [P, 2 * N], U8, N)
+        nc.sync.dma_start(w1_codes[:].bitcast(I32), w1_words[0].bitcast(I32))
         for q in range(4):
-            load_rows(nc.scalar, w1_plane, w1_scales[0], q)
-        for half in range(2):
-            for which, lst in enumerate((offs_l, two_l)):
-                part = lst[:, half * HALF // 16 : (half + 1) * HALF // 16]
-                nc.vector.tensor_copy(xw[which][half][:], xw_win[:].indirect(part))
-                nc.vector.tensor_copy(xs[which][half][:], xs_win[:].indirect(part))
-                product(which, dealt[which], half)
+            load_rows(nc.sync, w1_plane, w1_scales[0], q)
 
-        bias = tile("bias", [P, 4], F32)
-        nc.vector.scalar_tensor_tensor(bias[:], slope, -1.0, thresh, ALU.mult, ALU.mult)
-
-        z = [tile("z%d" % i, [P, HALF, PACK], BF16) for i in range(2)]
         z_codes = tile("z_codes", [P, S], U32)
         z_plane = tile("z_plane", [P, S], U8)
+        zt = [tile("zt%d" % i, [P, 2, P, 2], BF16) for i in range(2)]
+        z = [tile("z%d" % i, [P, HALF, PACK], BF16) for i in range(2)]
+        turned = [ps.tile([P, 2, HALF], F32, name="turned%d" % i, tag="b%d" % (5 + i)) for i in range(2)]
         for half in range(2):
-            nc.vector.scalar_tensor_tensor(
-                z[half][:],
-                acc[half][:].rearrange("p t j -> p j t"),
-                0.0625,
-                gain[:].unsqueeze(1).to_broadcast([P, HALF, PACK]),
-                ALU.mult,
-                ALU.mult,
+            for part in range(2):
+                ms = slice(part * P // 2, (part + 1) * P // 2)
+                nc.vector.tensor_tensor(
+                    zt[half][:, :, ms, :],
+                    acc[half][part][:].rearrange("p (m u e) -> p u m e", u=2, e=2),
+                    gain_row[:, :, ms, :],
+                    ALU.mult,
+                )
+            pairs = zt[half][:].rearrange("p u m e -> p (u m e)").bitcast(F32)
+            for u in range(2):
+                nc.tensor.transpose(turned[half][:, u, :], pairs[:, u * P : (u + 1) * P], ident[:])
+        for half in range(2):
+            nc.vector.tensor_copy(
+                z[half][:].rearrange("p j t -> p (j t)").bitcast(F32).rearrange("p (j u) -> p j u", u=2),
+                turned[half][:].rearrange("p u j -> p j u"),
             )
-        for half in range(2):
             cols = slice(half * HALF, (half + 1) * HALF)
             nc.vector.quantize_mx(
                 out=z_codes[:, cols].bitcast(FP8X4),
@@ -150,7 +164,10 @@ def tile_picked_mttonecpx_none_p_kernel(
                 in_=z[half][:].rearrange("p j t -> p (j t)"),
             )
 
-        bank = [ps.tile([P, S], F32, name="bank%d" % i) for i in range(4)]
+        bias = tile("bias", [P, 4], F32)
+        nc.vector.scalar_tensor_tensor(bias[:], slope, -1.0, thresh, ALU.mult, ALU.mult)
+
+        bank = [ps.tile([P, S], F32, name="bank%d" % i, tag="b%d" % (0, 7, 1, 2)[i]) for i in range(4)]
 
         def dense(c, cols):
             nc.tensor.matmul_mx(
@@ -168,7 +185,7 @@ def tile_picked_mttonecpx_none_p_kernel(
         for c in range(1, 4):
             dense(c, slice(0, S))
 
-        h2 = [tile("h2_%d" % c, [P, S], F32) for c in range(4)]
+        h2 = [tile("h2_%d" % c, [P, 2 * S], F32) for c in range(4)]
         sg = [tile("sg_%d" % c, [P, S], F32) for c in range(4)]
         st = [tile("st_%d" % c, [P, S], F32) for c in range(4)]
         pa = [tile("pa_%d" % c, [P, W], F32) for c in range(4)]
@@ -178,16 +195,15 @@ def tile_picked_mttonecpx_none_p_kernel(
         res = [tile("res_%d" % c, [P, S], F32) for c in range(4)]
 
         def gate(c):
-            nc.vector.tensor_copy(h2[c][:], bank[c][:])
-            for half in range(2):
-                nc.scalar.activation(
-                    out=sg[c][:, half * HALF : (half + 1) * HALF],
-                    in_=h2[c][:].indirect(n1_l[:, half * HALF // 16 : (half + 1) * HALF // 16]),
-                    func=ACT.Sigmoid,
-                    scale=rowvals[:, 0, c : c + 1],
-                    bias=bias[:, c : c + 1],
-                )
-            nc.vector.tensor_tensor(st[c][:], h2[c][:], sg[c][:], ALU.mult)
+            nc.vector.tensor_copy(h2[c][:, :S], bank[c][:])
+            nc.scalar.activation(
+                out=sg[c][:],
+                in_=h2[c][:].indirect(n1_l[:]),
+                func=ACT.Sigmoid,
+                scale=rowvals[:, 0, c : c + 1],
+                bias=bias[:, c : c + 1],
+            )
+            nc.vector.tensor_tensor(st[c][:], h2[c][:, :S], sg[c][:], ALU.mult)
 
         def pair(c):
             nc.scalar.activation(out=pa[c][:], in_=st[c][:].indirect(n2_l[:]), func=ACT.Copy)

@@ -46,7 +46,7 @@ def tile_picked_mttonecpx_none_p_kernel(
 
         def load_blocks(win, rows):
             words = rows.bitcast(I32)
-            nc.sync.dma_start(win[:].bitcast(I32), words.unsqueeze(1).to_broadcast([16, 8, words.shape[1]]))
+            nc.scalar.dma_start(win[:].bitcast(I32), words.unsqueeze(1).to_broadcast([16, 8, words.shape[1]]))
 
         def load_rows(queue, plane, rows, q):
             four = rows[4 * q : 4 * q + 4, :].bitcast(I32)
@@ -83,6 +83,9 @@ def tile_picked_mttonecpx_none_p_kernel(
         with nc.allow_non_contiguous_dma(reason="one value a row, one row a partition"):
             nc.sync.dma_start(slope, sl.rearrange("(c p) o -> p (c o)", p=P))
             nc.sync.dma_start(thresh, th.rearrange("(c p) o -> p (c o)", p=P))
+
+        warm = tile("warm", [P, 1], F32)
+        nc.scalar.activation(out=warm[:], in_=ident[:, 0:1], func=ACT.Sigmoid)
 
         gain_bank = ps.tile([P, PACK, P], F32, name="gain_bank", tag="b0")
         for t in range(PACK):
@@ -153,7 +156,7 @@ def tile_picked_mttonecpx_none_p_kernel(
             for u in range(2):
                 nc.tensor.transpose(turned[half][:, u, :], pairs[:, u * P : (u + 1) * P], ident[:])
         for half in range(2):
-            nc.vector.tensor_copy(
+            nc.scalar.copy(
                 z[half][:].rearrange("p j t -> p (j t)").bitcast(F32).rearrange("p (j u) -> p j u", u=2),
                 turned[half][:].rearrange("p u j -> p j u"),
             )
@@ -167,11 +170,10 @@ def tile_picked_mttonecpx_none_p_kernel(
         bias = tile("bias", [P, 4], F32)
         nc.vector.scalar_tensor_tensor(bias[:], slope, -1.0, thresh, ALU.mult, ALU.mult)
 
-        bank = [ps.tile([P, S], F32, name="bank%d" % i, tag="b%d" % (0, 7, 1, 2)[i]) for i in range(4)]
-
-        def dense(c, cols):
+        def dense(c, cols, tag):
+            bank = ps.tile([P, cols.stop - cols.start], F32, name="h2_bank%d_%d" % (c, cols.start), tag=tag)
             nc.tensor.matmul_mx(
-                out=bank[c][:, cols],
+                out=bank[:],
                 lhsT=w1_codes[:, 2 * P * c : 2 * P * (c + 1)].bitcast(FP4X4),
                 lhsT_scale=w1_plane[:, P * c : P * (c + 1)],
                 rhs=z_codes[:, cols].bitcast(FP8X4),
@@ -179,11 +181,7 @@ def tile_picked_mttonecpx_none_p_kernel(
                 start=True,
                 stop=True,
             )
-
-        dense(0, slice(0, HALF))
-        dense(0, slice(HALF, S))
-        for c in range(1, 4):
-            dense(c, slice(0, S))
+            nc.vector.tensor_copy(h2[c][:, cols], bank[:])
 
         h2 = [tile("h2_%d" % c, [P, 2 * S], F32) for c in range(4)]
         sg = [tile("sg_%d" % c, [P, S], F32) for c in range(4)]
@@ -194,8 +192,12 @@ def tile_picked_mttonecpx_none_p_kernel(
         rb = [tile("rb_%d" % c, [P, W], F32) for c in range(4)]
         res = [tile("res_%d" % c, [P, S], F32) for c in range(4)]
 
+        dense(0, slice(0, HALF), "b0")
+        dense(0, slice(HALF, S), "b7")
+        for c in range(1, 4):
+            dense(c, slice(0, S), "b%d" % c)
+
         def gate(c):
-            nc.vector.tensor_copy(h2[c][:, :S], bank[c][:])
             nc.scalar.activation(
                 out=sg[c][:],
                 in_=h2[c][:].indirect(n1_l[:]),

@@ -52,9 +52,9 @@ def tile_picked_mttonecpx_none_p_kernel(
             four = rows[4 * q : 4 * q + 4, :].bitcast(I32)
             queue.dma_start(plane[32 * q : 32 * (q + 1), :].bitcast(I32), four.unsqueeze(0).to_broadcast([8] + list(four.shape)))
 
-        ds_win = tile("ds_win", [P, G], U8)
+        ds_win = placed("ds_win", [P, G], U8, 0)
         dw_win = tile("dw_win", [P, G], U32)
-        sc_got = placed("sc_got", [P, 2 * H + 2 * S], U8, 0)
+        sc_got = tile("sc_got", [P, 2 * H + 2 * S], U8)
         xs_win = tile("xs_win", [P, T], U8)
         xw_win = tile("xw_win", [P, T], U32)
         plane = tile("plane", [P, 2 * H + 2 * S], U8)
@@ -83,9 +83,6 @@ def tile_picked_mttonecpx_none_p_kernel(
         with nc.allow_non_contiguous_dma(reason="one value a row, one row a partition"):
             nc.sync.dma_start(slope, sl.rearrange("(c p) o -> p (c o)", p=P))
             nc.sync.dma_start(thresh, th.rearrange("(c p) o -> p (c o)", p=P))
-
-        warm = tile("warm", [P, 1], F32)
-        nc.scalar.activation(out=warm[:], in_=ident[:, 0:1], func=ACT.Sigmoid)
 
         gain_bank = ps.tile([P, PACK, P], F32, name="gain_bank", tag="b0")
         for t in range(PACK):
@@ -156,7 +153,7 @@ def tile_picked_mttonecpx_none_p_kernel(
             for u in range(2):
                 nc.tensor.transpose(turned[half][:, u, :], pairs[:, u * P : (u + 1) * P], ident[:])
         for half in range(2):
-            nc.scalar.copy(
+            nc.vector.tensor_copy(
                 z[half][:].rearrange("p j t -> p (j t)").bitcast(F32).rearrange("p (j u) -> p j u", u=2),
                 turned[half][:].rearrange("p u j -> p j u"),
             )

@@ -54,11 +54,11 @@ def tile_picked_mttonecpx_none_p_kernel(
 
         ds_win = placed("ds_win", [P, G], U8, 0)
         dw_win = tile("dw_win", [P, G], U32)
-        sc_got = tile("sc_got", [P, 2 * H + 2 * S], U8)
         xs_win = tile("xs_win", [P, T], U8)
         xw_win = tile("xw_win", [P, T], U32)
-        plane = tile("plane", [P, 2 * H + 2 * S], U8)
-        nc.vector.memset(plane[:].bitcast(I32), 0)
+        plane = [tile("plane0", [P, 2 * S + H], U8), tile("plane1", [P, H], U8)]
+        for which in range(2):
+            nc.vector.memset(plane[which][:].bitcast(I32), 0)
         gain = tile("gain", [P, PACK], F32)
         nc.gpsimd.dma_start(gain[:], gn.rearrange("(p t) o -> p (t o)", t=PACK))
         ident = tile("ident", [P, P], F32)
@@ -77,12 +77,6 @@ def tile_picked_mttonecpx_none_p_kernel(
         n3_l = load_list("n3_l", n3)
         n4_l = load_list("n4_l", n4)
         n5_l = load_list("n5_l", n5)
-        rowvals = tile("rowvals", [P, 2, 8], F32)
-        slope = rowvals[:, 0, 0:4]
-        thresh = rowvals[:, 1, 0:4]
-        with nc.allow_non_contiguous_dma(reason="one value a row, one row a partition"):
-            nc.sync.dma_start(slope, sl.rearrange("(c p) o -> p (c o)", p=P))
-            nc.sync.dma_start(thresh, th.rearrange("(c p) o -> p (c o)", p=P))
 
         gain_bank = ps.tile([P, PACK, P], F32, name="gain_bank", tag="b0")
         for t in range(PACK):
@@ -92,12 +86,18 @@ def tile_picked_mttonecpx_none_p_kernel(
             out=gain_row[:], in_=gain_bank[:].rearrange("p (u e) m -> p u m e", e=2), func=ACT.Copy, scale=0.0625
         )
 
-        nc.vector.tensor_copy(sc_got[:, 2 * H : 2 * H + S], xs_win[:].indirect(offs_l[:]))
-        nc.vector.tensor_copy(sc_got[:, 2 * H + S :], xs_win[:].indirect(two_l[:]))
-        nc.vector.tensor_copy(sc_got[:, :H], ds_win[:].indirect(k1_l[:]))
-        nc.vector.tensor_copy(sc_got[:, H : 2 * H], ds_win[:].indirect(k2_l[:]))
-        for s in range(4):
-            nc.sync.dma_start(plane[s:P:32, :].bitcast(I32), sc_got[8 * s : P : 32, :].bitcast(I32))
+        def move_rows(dst, src):
+            for s in range(4):
+                nc.sync.dma_start(dst[s:P:32, :].bitcast(I32), src[8 * s : P : 32, :].bitcast(I32))
+
+        got0 = tile("got0", [P, 2 * S + H], U8)
+        got1 = tile("got1", [P, H], U8)
+        nc.vector.tensor_copy(got0[:, H : H + S], xs_win[:].indirect(offs_l[:]))
+        nc.vector.tensor_copy(got0[:, H + S :], xs_win[:].indirect(two_l[:]))
+        nc.vector.tensor_copy(got0[:, :H], ds_win[:].indirect(k1_l[:]))
+        move_rows(plane[0], got0)
+        nc.vector.tensor_copy(got1[:], ds_win[:].indirect(k2_l[:]))
+        move_rows(plane[1], got1)
 
         xw = [tile("xw%d" % i, [P, S], U32) for i in range(2)]
         nc.vector.tensor_copy(xw[0][:], xw_win[:].indirect(offs_l[:]))
@@ -108,14 +108,14 @@ def tile_picked_mttonecpx_none_p_kernel(
         acc = [[ps.tile([P, HH], F32, name="acc%d%d" % (i, j), tag="b%d" % (1 + 2 * i + j)) for j in range(2)] for i in range(2)]
 
         def product(which, half, part, words):
-            x0 = 2 * H + which * S + half * HALF
-            d0 = which * H + part * HH
+            x0 = H + which * S + half * HALF
+            d0 = part * HH
             nc.tensor.matmul_mx(
                 out=acc[half][part][:],
                 lhsT=xw[which][:, half * HALF : (half + 1) * HALF].bitcast(FP8X4),
-                lhsT_scale=plane[:, x0 : x0 + HALF],
+                lhsT_scale=plane[0][:, x0 : x0 + HALF],
                 rhs=words.bitcast(FP8X4),
-                rhs_scale=plane[:, d0 : d0 + HH],
+                rhs_scale=plane[which][:, d0 : d0 + HH],
                 start=(which == 0),
                 stop=(which == 1),
             )
@@ -129,6 +129,12 @@ def tile_picked_mttonecpx_none_p_kernel(
             for half in range(2):
                 product(1, half, part, dw2[part][:])
 
+        rowvals = placed("rowvals", [P, 2, 8], F32, 3 * N)
+        slope = rowvals[:, 0, 0:4]
+        thresh = rowvals[:, 1, 0:4]
+        with nc.allow_non_contiguous_dma(reason="one value a row, one row a partition"):
+            nc.sync.dma_start(slope, sl.rearrange("(c p) o -> p (c o)", p=P))
+            nc.sync.dma_start(thresh, th.rearrange("(c p) o -> p (c o)", p=P))
         w1_plane = placed("w1_plane", [P, N], U8, 0)
         w1_codes = placed("w1_codes", [P, 2 * N], U8, N)
         nc.sync.dma_start(w1_codes[:].bitcast(I32), w1_words[0].bitcast(I32))

from contextlib import ExitStack

import concourse.mybir as mybir
from concourse.masks import make_identity

K, T, S, N, G, H, W = 512, 1024, 256, 512, 2048, 512, 128
FLOPS = 2 * (2 * K * H * S + H * N * S)

F32 = mybir.dt.float32
BF16 = mybir.dt.bfloat16
I32 = mybir.dt.int32
U32 = mybir.dt.uint32
U16 = mybir.dt.uint16
U8 = mybir.dt.uint8
FP8X4 = mybir.dt.float8_e4m3fn_x4
FP4X4 = mybir.dt.float4_e2m1fn_x4
ALU = mybir.AluOpType
ACT = mybir.ActivationFunctionType

P = 128
PACK = 4
HALF = S // 2


def tile_picked_mttonecpx_none_p_kernel(
    tc, x_words, x_scales, d_words, d_scales, gn, w1_words, w1_scales, sl, th,
    offs, k1, two, k2, n1, n2, n3, n4, n5, out,
):
    nc = tc.nc
    with ExitStack() as ctx:
        sb = ctx.enter_context(tc.tile_pool(name="sb", bufs=1))
        ps = ctx.enter_context(tc.psum_pool(name="ps", bufs=1))

        reuse = ctx.enter_context(tc.tile_pool(name="reuse", bufs=1))

        def tile(name, shape, dtype):
            return sb.tile(shape, dtype, name=name, align_bytes=64)

        def placed(name, shape, dtype, offset):
            return reuse.tile(shape, dtype, name=name, align_bytes=64, offset=offset)

        def load_list(name, src):
            t = tile(name, list(src.shape), U16)
            nc.sync.dma_start(t[:], src)
            return t

        def load_blocks(win, rows):
            words = rows.bitcast(I32)
            nc.scalar.dma_start(win[:].bitcast(I32), words.unsqueeze(1).to_broadcast([16, 8, words.shape[1]]))

        def load_rows(queue, plane, rows, q):
            four = rows[4 * q : 4 * q + 4, :].bitcast(I32)
            queue.dma_start(plane[32 * q : 32 * (q + 1), :].bitcast(I32), four.unsqueeze(0).to_broadcast([8] + list(four.shape)))

        ds_win = placed("ds_win", [P, G], U8, 0)
        dw_win = tile("dw_win", [P, G], U32)
        xs_win = tile("xs_win", [P, T], U8)
        xw_win = tile("xw_win", [P, T], U32)
        plane = [tile("plane0", [P, 2 * S + H], U8), tile("plane1", [P, H], U8)]
        for which in range(2):
            nc.vector.memset(plane[which][:].bitcast(I32), 0)
        gain = tile("gain", [P, PACK], F32)
        nc.gpsimd.dma_start(gain[:], gn.rearrange("(p t) o -> p (t o)", t=PACK))
        ident = tile("ident", [P, P], F32)
        make_identity(nc, ident[:])

        offs_l = load_list("offs_l", offs)
        load_blocks(xs_win, x_scales[0])
        two_l = load_list("two_l", two)
        k1_l = load_list("k1_l", k1)
        load_blocks(ds_win, d_scales[0])
        k2_l = load_list("k2_l", k2)
        nc.sync.dma_start(xw_win[:].bitcast(I32), x_words[0].rearrange("p c r -> p (c r)").bitcast(I32))
        nc.sync.dma_start(dw_win[:].bitcast(I32), d_words[0].rearrange("p c r -> p (c r)").bitcast(I32))
        n1_l = load_list("n1_l", n1)
        n2_l = load_list("n2_l", n2)
        n3_l = load_list("n3_l", n3)
        n4_l = load_list("n4_l", n4)
        n5_l = load_list("n5_l", n5)

        gain_bank = ps.tile([P, PACK, P], F32, name="gain_bank", tag="b0")
        for t in range(PACK):
            nc.tensor.transpose(gain_bank[:, t, :], gain[:, t : t + 1].to_broadcast([P, P]), ident[:])
        gain_row = tile("gain_row", [P, 2, P, 2], F32)
        nc.scalar.activation(
            out=gain_row[:], in_=gain_bank[:].rearrange("p (u e) m -> p u m e", e=2), func=ACT.Copy, scale=0.0625
        )

        def move_rows(dst, src):
            for s in range(4):
                nc.sync.dma_start(dst[s:P:32, :].bitcast(I32), src[8 * s : P : 32, :].bitcast(I32))

        got0 = tile("got0", [P, 2 * S + H], U8)
        got1 = tile("got1", [P, H], U8)
        nc.vector.tensor_copy(got0[:, H : H + S], xs_win[:].indirect(offs_l[:]))
        nc.vector.tensor_copy(got0[:, H + S :], xs_win[:].indirect(two_l[:]))
        nc.vector.tensor_copy(got0[:, :H], ds_win[:].indirect(k1_l[:]))
        move_rows(plane[0], got0)
        nc.vector.tensor_copy(got1[:], ds_win[:].indirect(k2_l[:]))
        move_rows(plane[1], got1)

        xw = [tile("xw%d" % i, [P, S], U32) for i in range(2)]
        nc.vector.tensor_copy(xw[0][:], xw_win[:].indirect(offs_l[:]))
        nc.vector.tensor_copy(xw[1][:], xw_win[:].indirect(two_l[:]))
        HH = H // 2
        dw1 = tile("dw1", [P, H], U32)
        dw2 = [tile("dw2_%d" % i, [P, HH], U32) for i in range(2)]
        acc = [[ps.tile([P, HH], F32, name="acc%d%d" % (i, j), tag="b%d" % (1 + 2 * i + j)) for j in range(2)] for i in range(2)]

        def product(which, half, part, words):
            x0 = H + which * S + half * HALF
            d0 = part * HH
            nc.tensor.matmul_mx(
                out=acc[half][part][:],
                lhsT=xw[which][:, half * HALF : (half + 1) * HALF].bitcast(FP8X4),
                lhsT_scale=plane[0][:, x0 : x0 + HALF],
                rhs=words.bitcast(FP8X4),
                rhs_scale=plane[which][:, d0 : d0 + HH],
                start=(which == 0),
                stop=(which == 1),
            )

        nc.vector.tensor_copy(dw1[:], dw_win[:].indirect(k1_l[:]))
        for part in range(2):
            for half in range(2):
                product(0, half, part, dw1[:, part * HH : (part + 1) * HH])
        for part in range(2):
            nc.vector.tensor_copy(dw2[part][:], dw_win[:].indirect(k2_l[:, part * HH // 16 : (part + 1) * HH // 16]))
            for half in range(2):
                product(1, half, part, dw2[part][:])

        rowvals = placed("rowvals", [P, 2, 8], F32, 3 * N)
        slope = rowvals[:, 0, 0:4]
        thresh = rowvals[:, 1, 0:4]
        with nc.allow_non_contiguous_dma(reason="one value a row, one row a partition"):
            nc.sync.dma_start(slope, sl.rearrange("(c p) o -> p (c o)", p=P))
            nc.sync.dma_start(thresh, th.rearrange("(c p) o -> p (c o)", p=P))
        w1_plane = placed("w1_plane", [P, N], U8, 0)
        w1_codes = placed("w1_codes", [P, 2 * N], U8, N)
        nc.sync.dma_start(w1_codes[:].bitcast(I32), w1_words[0].bitcast(I32))
        for q in range(4):
            load_rows(nc.sync, w1_plane, w1_scales[0], q)

        z_codes = tile("z_codes", [P, S], U32)
        z_plane = tile("z_plane", [P, S], U8)
        zt = [tile("zt%d" % i, [P, 2, P, 2], BF16) for i in range(2)]
        z = [tile("z%d" % i, [P, HALF, PACK], BF16) for i in range(2)]
        turned = [ps.tile([P, 2, HALF], F32, name="turned%d" % i, tag="b%d" % (5 + i)) for i in range(2)]
        for half in range(2):
            for part in range(2):
                ms = slice(part * P // 2, (part + 1) * P // 2)
                nc.vector.tensor_tensor(
                    zt[half][:, :, ms, :],
                    acc[half][part][:].rearrange("p (m u e) -> p u m e", u=2, e=2),
                    gain_row[:, :, ms, :],
                    ALU.mult,
                )
            pairs = zt[half][:].rearrange("p u m e -> p (u m e)").bitcast(F32)
            for u in range(2):
                nc.tensor.transpose(turned[half][:, u, :], pairs[:, u * P : (u + 1) * P], ident[:])
        for half in range(2):
            nc.vector.tensor_copy(
                z[half][:].rearrange("p j t -> p (j t)").bitcast(F32).rearrange("p (j u) -> p j u", u=2),
                turned[half][:].rearrange("p u j -> p j u"),
            )
            cols = slice(half * HALF, (half + 1) * HALF)
            nc.vector.quantize_mx(
                out=z_codes[:, cols].bitcast(FP8X4),
                scales=z_plane[:, cols],
                in_=z[half][:].rearrange("p j t -> p (j t)"),
            )

        bias = tile("bias", [P, 4], F32)
        nc.vector.scalar_tensor_tensor(bias[:], slope, -1.0, thresh, ALU.mult, ALU.mult)

        def dense(c, cols, tag):
            bank = ps.tile([P, cols.stop - cols.start], F32, name="h2_bank%d_%d" % (c, cols.start), tag=tag)
            nc.tensor.matmul_mx(
                out=bank[:],
                lhsT=w1_codes[:, 2 * P * c : 2 * P * (c + 1)].bitcast(FP4X4),
                lhsT_scale=w1_plane[:, P * c : P * (c + 1)],
                rhs=z_codes[:, cols].bitcast(FP8X4),
                rhs_scale=z_plane[:, cols],
                start=True,
                stop=True,
            )
            nc.vector.tensor_copy(h2[c][:, cols], bank[:])

        h2 = [tile("h2_%d" % c, [P, 2 * S], F32) for c in range(4)]
        sg = [tile("sg_%d" % c, [P, S], F32) for c in range(4)]
        st = [tile("st_%d" % c, [P, S], F32) for c in range(4)]
        pa = [tile("pa_%d" % c, [P, W], F32) for c in range(4)]
        pb = [tile("pb_%d" % c, [P, W], F32) for c in range(4)]
        ra = [tile("ra_%d" % c, [P, W], F32) for c in range(4)]
        rb = [tile("rb_%d" % c, [P, W], F32) for c in range(4)]
        res = [tile("res_%d" % c, [P, S], F32) for c in range(4)]

        dense(0, slice(0, HALF), "b0")
        dense(0, slice(HALF, S), "b7")
        for c in range(1, 4):
            dense(c, slice(0, S), "b%d" % c)

        def gate(c):
            nc.scalar.activation(
                out=sg[c][:],
                in_=h2[c][:].indirect(n1_l[:]),
                func=ACT.Sigmoid,
                scale=rowvals[:, 0, c : c + 1],
                bias=bias[:, c : c + 1],
            )
            nc.vector.tensor_tensor(st[c][:], h2[c][:, :S], sg[c][:], ALU.mult)

        def pair(c):
            nc.scalar.activation(out=pa[c][:], in_=st[c][:].indirect(n2_l[:]), func=ACT.Copy)
            nc.scalar.activation(out=pb[c][:], in_=st[c][:].indirect(n3_l[:]), func=ACT.Copy)
            nc.vector.tensor_tensor(ra[c][:], pa[c][:], pb[c][:], ALU.max)
            nc.vector.tensor_tensor(rb[c][:], pa[c][:], pb[c][:], ALU.subtract)

        def place(c):
            nc.scalar.activation(out=res[c][:].indirect(n4_l[:]), in_=ra[c][:], func=ACT.Copy)
            nc.scalar.activation(out=res[c][:].indirect(n5_l[:]), in_=rb[c][:], func=ACT.Copy)
            nc.sync.dma_start(out[c * P : (c + 1) * P, :], res[c][:])

        for step in range(6):
            if step < 4:
                gate(step)
            if 1 <= step < 5:
                pair(step - 1)
            if step >= 2:
                place(step - 2)
